import numpy as np
import ml_dtypes


def mxq(x, axis, fmt="e4m3"):
    dtype, down = {"e4m3": (ml_dtypes.float8_e4m3fn, 7), "e5m2": (ml_dtypes.float8_e5m2, 14)}[fmt]
    v = np.moveaxis(np.asarray(x, np.float32).astype(ml_dtypes.bfloat16).astype(np.float64), axis, -1)
    blocks = v.reshape(v.shape[:-1] + (-1, 32))
    amax = np.abs(blocks).max(-1, keepdims=True)
    byte = np.maximum(np.where(amax > 0, np.frexp(amax)[1] - 1 + 127, 0) - down, 1)
    scale = np.exp2(byte - 127.0)
    codes = (blocks / scale).astype(np.float32).astype(dtype).astype(np.float64)
    return np.moveaxis((codes * scale).reshape(v.shape), -1, axis)


WIDE = False


def mx_kscale(k):
    if not WIDE:
        return np.ones(k)
    levels = np.array([30, -30])
    if k % 512:
        return np.exp2(np.random.permutation(np.resize(levels, k // 32))).repeat(32)
    a = np.empty((k // 512, 16))
    for p in range(k // 512):
        a[p, :8] = np.random.permutation(np.resize(levels, 8))
        for g in range(8):
            far = levels[np.abs(levels - a[p, g]) >= 10]
            a[p, g + 8] = far[np.random.randint(len(far))]
    return np.exp2(a.ravel()).repeat(32)


def f64(x):
    return np.asarray(x).astype(np.float64)


def striped(idx):
    return np.tile(np.asarray(idx).reshape(-1, 16).T, (8, 1)).astype(np.uint16)


def unstriped(offs):
    return offs[:16].T.reshape(-1).astype(np.int64)


E2M1 = np.array([0.0, 0.5, 1.0, 1.5, 2.0, 3.0, 4.0, 6.0, -0.0, -0.5, -1.0, -1.5, -2.0, -3.0, -4.0, -6.0])


def pack_weight(w, fmt):
    k, n = w.shape
    w = f64(np.asarray(w, np.float32).astype(ml_dtypes.bfloat16)).reshape(k // 32, 32, n)
    amax = np.abs(w).max(1)
    if fmt in ("e4m3", "e5m2"):
        byte = np.frexp(amax)[1] - 1 + 127 - (7 if fmt == "e4m3" else 14)
    else:
        mant, ex = np.frexp(amax / 6.0)
        byte = np.where(mant > 0.5, ex, ex - 1) + 127
    byte = np.clip(np.where(amax > 0, byte, 1), 1, 254)
    scaled = (w * np.exp2(127.0 - byte)[:, None, :]).reshape(k, n).astype(np.float32)
    by_word = np.ascontiguousarray(scaled.reshape(k // 512, 128, 4, n).transpose(0, 1, 3, 2))
    if fmt in ("e4m3", "e5m2"):
        words = by_word.astype(ml_dtypes.float8_e4m3fn if fmt == "e4m3" else ml_dtypes.float8_e5m2).view(np.uint8)
    else:
        c = by_word.astype(ml_dtypes.float4_e2m1fn).view(np.uint8) & 0xF
        words = (c[..., 0::2] | (c[..., 1::2] << 4)).reshape(k // 512, 128, 2 * n)
    return np.ascontiguousarray(words), np.ascontiguousarray(byte.astype(np.uint8).reshape(k // 512, 16, n))


def unpack_weight(words, scales, fmt):
    g, _, n = scales.shape
    words = np.ascontiguousarray(words).reshape(g, 128, n, -1)
    if fmt in ("e4m3", "e5m2"):
        vals = words.view(ml_dtypes.float8_e4m3fn if fmt == "e4m3" else ml_dtypes.float8_e5m2).astype(np.float64)
    else:
        nib = np.empty((g, 128, n, 4), np.uint8)
        nib[..., 0::2] = words & 0xF
        nib[..., 1::2] = words >> 4
        vals = E2M1[nib]
    vals = vals * np.repeat(np.exp2(scales.astype(np.float64) - 127.0), 8, axis=1)[..., None]
    return vals.transpose(0, 1, 3, 2).reshape(g * 512, n)


K, T, J, R, C, N, E = 512, 2048, 256, 512, 512, 256, 1024


def setup_inputs():
    n = np.random.standard_normal
    idx = np.random.permutation(T)[:J]
    idx2 = np.random.permutation(T)[:J]
    idx3 = np.random.permutation(C)[:J]
    idx4 = np.random.permutation(C)[:J]
    idx5 = np.random.permutation(E)[:J]
    fk = mx_kscale(K)
    fr = mx_kscale(R)
    xtp = pack_weight(n((K, T)) / fk[:, None], "e4m3")
    wp = pack_weight(n((K, R)) * 1 / np.sqrt(K) * fk[:, None] * fr, "e2m1")
    wbp = pack_weight(n((R, N)) * 1 / np.sqrt(R) / fr[:, None], "e5m2")
    wsp = pack_weight(n((K, N)) * 1 / np.sqrt(K) * fk[:, None], "e5m2")
    return {
        "xt_words": xtp[0],
        "xt_scales": xtp[1],
        "w_words": wp[0],
        "w_scales": wp[1],
        "wb_words": wbp[0],
        "wb_scales": wbp[1],
        "ws_words": wsp[0],
        "ws_scales": wsp[1],
        "tz": (n((N, E))).astype(np.float32),
        "offs": striped(idx),
        "offs2": striped(idx2),
        "offs3": striped(idx3),
        "offs4": striped(idx4),
        "offs5": striped(idx5),
    }


def reference(xt_words, xt_scales, w_words, w_scales, wb_words, wb_scales, ws_words, ws_scales, tz, offs, offs2, offs3, offs4, offs5):
    idx = unstriped(offs)
    idx2 = unstriped(offs2)
    idx3 = unstriped(offs3)
    idx4 = unstriped(offs4)
    idx5 = unstriped(offs5)
    xtu = unpack_weight(xt_words, xt_scales, "e4m3")
    wu = unpack_weight(w_words, w_scales, "e2m1")
    wbu = unpack_weight(wb_words, wb_scales, "e5m2")
    wsu = unpack_weight(ws_words, ws_scales, "e5m2")
    xtidxg = xtu[:, idx]
    a = wu.T @ xtidxg
    xtidx2g = xtu[:, idx2]
    b = wu.T @ xtidx2g
    pw = np.zeros((R, C))
    pw[:, idx3] = a
    hid = np.abs(pw[:, idx4] - b)
    hidq = mxq(hid, 0, "e4m3")
    p = wbu.T @ hidq + wsu.T @ xtidx2g
    y = p + f64(tz)[:, idx5]
    return y

@@ -1,0 +1,140 @@
+from contextlib import ExitStack
+
+import concourse.mybir as mybir
+
+K, T, J, R, C, N, E = 512, 2048, 256, 512, 512, 256, 1024
+FLOPS = 2 * J * (2 * K * R + R * N + K * N)
+
+F32 = mybir.dt.float32
+BF16 = mybir.dt.bfloat16
+I32 = mybir.dt.int32
+U32 = mybir.dt.uint32
+U16 = mybir.dt.uint16
+U8 = mybir.dt.uint8
+E4M3 = mybir.dt.float8_e4m3fn_x4
+E5M2 = mybir.dt.float8_e5m2_x4
+E2M1 = mybir.dt.float4_e2m1fn_x4
+ACT = mybir.ActivationFunctionType
+ALU = mybir.AluOpType
+P = 128
+PACK = 4
+
+
+def load_scale_rows(queue, plane, scales):
+    for q in range(4):
+        queue.dma_start(out=plane[32 * q : 32 * q + 4, :].bitcast(I32), in_=scales[0, 4 * q : 4 * q + 4, :].bitcast(I32))
+
+
+def tile_list_tied_board_skip_tabled_kernel(tc, xt_words, xt_scales, w_words, w_scales, wb_words, wb_scales,
+                                                ws_words, ws_scales, tz, offs, offs2, offs3, offs4, offs5, out):
+    nc = tc.nc
+    with ExitStack() as ctx:
+        sb = ctx.enter_context(tc.tile_pool(name="sb", bufs=1))
+        ps = ctx.enter_context(tc.psum_pool(name="ps", bufs=1))
+
+        def tile(shape, dtype, name):
+            return sb.tile(shape, dtype, name=name, align_bytes=64)
+
+        lists = [sb.tile([P, J // 16], U16, name="list%d" % i) for i in range(5)]
+        x_words = tile([P, T], U32, "x_words")
+        x_bytes = tile([P, T], U8, "x_bytes")
+        w_raw = tile([P, 2 * R], U8, "w_raw")
+        w_raw_bytes = tile([P, R], U8, "w_raw_bytes")
+        o_bytes = tile([P, 2 * N], U8, "o_bytes")
+        wb_sb = tile([P, N], U32, "wb_sb")
+        ws_sb = tile([P, N], U32, "ws_sb")
+        tz_sb = [tile([P, E], F32, "tz%d" % h) for h in range(2)]
+        board = [tile([P, C], F32, "board%d" % t) for t in range(PACK)]
+
+        nc.vector.memset(w_raw_bytes[:].bitcast(I32), 0)
+        nc.vector.memset(x_bytes[:].bitcast(I32), 0)
+        nc.vector.memset(o_bytes[:].bitcast(I32), 0)
+        for t in range(PACK):
+            nc.vector.memset(board[t][:], 0.0)
+
+        nc.sync.dma_start(lists[0][:], offs)
+        nc.sync.dma_start(out=w_raw[:].bitcast(I32), in_=w_words[0].bitcast(I32))
+        nc.sync.dma_start(out=x_words[:].bitcast(I32), in_=xt_words[0].rearrange("p n t -> p (n t)").bitcast(I32))
+        load_scale_rows(nc.scalar, w_raw_bytes[:], w_scales)
+        load_scale_rows(nc.sync, x_bytes[:], xt_scales)
+        nc.sync.dma_start(lists[2][:], offs3)
+        nc.sync.dma_start(lists[1][:], offs2)
+        nc.sync.dma_start(lists[3][:], offs4)
+        nc.sync.dma_start(out=ws_sb[:].bitcast(I32), in_=ws_words[0].rearrange("p n t -> p (n t)").bitcast(I32))
+        load_scale_rows(nc.sync, o_bytes[:, N : 2 * N], ws_scales)
+        nc.sync.dma_start(lists[4][:], offs5)
+        for h in range(2):
+            nc.sync.dma_start(out=tz_sb[h][:], in_=tz[P * h : P * (h + 1), :])
+        nc.sync.dma_start(out=wb_sb[:].bitcast(I32), in_=wb_words[0].rearrange("p n t -> p (n t)").bitcast(I32))
+        load_scale_rows(nc.sync, o_bytes[:, 0:N], wb_scales)
+
+        w_sb = tile([P, 2 * R], U8, "w_sb")
+        w_bytes = tile([P, R], U8, "w_bytes")
+        nc.scalar.copy(out=w_sb[:].bitcast(U16).rearrange("p (t m) -> p t m", t=PACK),
+                       in_=w_raw[:].bitcast(U16).rearrange("p (m t) -> p t m", t=PACK))
+        nc.vector.tensor_copy(out=w_bytes[:].rearrange("p (t m) -> p t m", t=PACK),
+                              in_=w_raw_bytes[:].rearrange("p (m t) -> p t m", t=PACK))
+
+        g_words = [tile([P, J], U32, "g_words%d" % i) for i in range(2)]
+        g_bytes = [tile([P, J], U8, "g_bytes%d" % i) for i in range(2)]
+
+        def first_matrix(dst, t, i):
+            nc.tensor.matmul_mx(out=dst, lhsT=w_sb[:, 2 * P * t : 2 * P * (t + 1)].bitcast(E2M1),
+                                lhsT_scale=w_bytes[:, P * t : P * (t + 1)],
+                                rhs=g_words[i][:].bitcast(E4M3), rhs_scale=g_bytes[i][:], start=True, stop=True)
+
+        nc.vector.tensor_copy(g_bytes[0][:], x_bytes[:].indirect(lists[0][:]))
+        nc.vector.tensor_copy(g_words[0][:], x_words[:].indirect(lists[0][:]))
+        a_ps = [ps.tile([P, J], F32, name="a_ps%d" % t) for t in range(PACK)]
+        for t in range(PACK):
+            first_matrix(a_ps[t][:], t, 0)
+
+        nc.vector.tensor_copy(g_bytes[1][:], x_bytes[:].indirect(lists[1][:]))
+        nc.vector.tensor_copy(g_words[1][:], x_words[:].indirect(lists[1][:]))
+        b_ps = [ps.tile([P, 2, J], F32, name="b_ps%d" % u) for u in range(2)]
+        for t in range(PACK):
+            first_matrix(b_ps[t // 2][:, t % 2, :], t, 1)
+        p_ps = [ps.tile([P, J], F32, name="p_ps%d" % h) for h in range(2)]
+        for h in range(2):
+            nc.tensor.matmul_mx(out=p_ps[h][:], lhsT=ws_sb[:, P * h : P * (h + 1)].bitcast(E5M2),
+                                lhsT_scale=o_bytes[:, N + P * h : N + P * (h + 1)],
+                                rhs=g_words[1][:].bitcast(E4M3), rhs_scale=g_bytes[1][:], start=True, stop=False)
+
+        a_sb = [tile([P, J], F32, "a_sb%d" % t) for t in range(PACK)]
+        seen = [tile([P, J], F32, "seen%d" % t) for t in range(PACK)]
+        diff = tile([P, PACK, J], F32, "diff")
+        for t in range(PACK):
+            if t % 2 == 0:
+                nc.scalar.copy(out=a_sb[t][:], in_=a_ps[t][:])
+                nc.scalar.activation(board[t][:].indirect(lists[2][:]), a_sb[t][:], ACT.Copy)
+            else:
+                nc.vector.tensor_copy(out=a_sb[t][:], in_=a_ps[t][:])
+                nc.vector.tensor_copy(board[t][:].indirect(lists[2][:]), a_sb[t][:])
+        for t in range(PACK):
+            if t % 2 == 0:
+                nc.scalar.activation(seen[t][:], board[t][:].indirect(lists[3][:]), ACT.Copy)
+            else:
+                nc.vector.tensor_copy(seen[t][:], board[t][:].indirect(lists[3][:]))
+        for t in range(PACK):
+            nc.vector.tensor_tensor(out=diff[:, t, :], in0=seen[t][:], in1=b_ps[t // 2][:, t % 2, :], op=ALU.subtract)
+
+        hid = tile([P, J, PACK], BF16, "hid")
+        half = J // 2
+        nc.scalar.activation(out=hid[:, 0:half, :], in_=diff[:, :, 0:half].rearrange("p t j -> p j t"), func=ACT.Abs)
+        upper = diff[:, :, half:J].rearrange("p t j -> p j t")
+        nc.vector.scalar_tensor_tensor(out=hid[:, half:J, :], in0=upper, scalar=-1.0, in1=upper, op0=ALU.mult, op1=ALU.max)
+        h_words = tile([P, J], U32, "h_words")
+        h_bytes = tile([P, J], U8, "h_bytes")
+        nc.vector.quantize_mx(out=h_words[:].bitcast(E4M3), scales=h_bytes[:], in_=hid[:].rearrange("p j t -> p (j t)"))
+
+        picked = [tile([P, J], F32, "picked%d" % h) for h in range(2)]
+        res = [tile([P, J], F32, "res%d" % h) for h in range(2)]
+        for h in range(2):
+            nc.tensor.matmul_mx(out=p_ps[h][:], lhsT=wb_sb[:, P * h : P * (h + 1)].bitcast(E5M2),
+                                lhsT_scale=o_bytes[:, P * h : P * (h + 1)],
+                                rhs=h_words[:].bitcast(E4M3), rhs_scale=h_bytes[:], start=False, stop=True)
+        for h in range(2):
+            nc.scalar.activation(picked[h][:], tz_sb[h][:].indirect(lists[4][:]), ACT.Copy)
+        for h in range(2):
+            nc.vector.tensor_tensor(out=res[h][:], in0=p_ps[h][:], in1=picked[h][:], op=ALU.add)
+            (nc.sync, nc.scalar)[h].dma_start(out=out[P * h : P * (h + 1), :], in_=res[h][:])

@@ -18,11 +18,13 @@ ACT = mybir.ActivationFunctionType
 ALU = mybir.AluOpType
 P = 128
 PACK = 4
+HALF = J // 2
+CUT = 64
 
 
-def load_scale_rows(queue, plane, scales):
+def load_scale_rows(queues, plane, scales):
     for q in range(4):
-        queue.dma_start(out=plane[32 * q : 32 * q + 4, :].bitcast(I32), in_=scales[0, 4 * q : 4 * q + 4, :].bitcast(I32))
+        queues[q].dma_start(out=plane[32 * q : 32 * q + 4, :].bitcast(I32), in_=scales[0, 4 * q : 4 * q + 4, :].bitcast(I32))
 
 
 def tile_list_tied_board_skip_tabled_kernel(tc, xt_words, xt_scales, w_words, w_scales, wb_words, wb_scales,
@@ -48,25 +50,26 @@ def tile_list_tied_board_skip_tabled_kernel(tc, xt_words, xt_scales, w_words, w_
 
         nc.vector.memset(w_raw_bytes[:].bitcast(I32), 0)
         nc.vector.memset(x_bytes[:].bitcast(I32), 0)
-        nc.vector.memset(o_bytes[:].bitcast(I32), 0)
+        nc.gpsimd.memset(o_bytes[:].bitcast(I32), 0)
         for t in range(PACK):
             nc.vector.memset(board[t][:], 0.0)
 
+        sync4 = [nc.sync] * 4
         nc.sync.dma_start(lists[0][:], offs)
-        nc.sync.dma_start(out=w_raw[:].bitcast(I32), in_=w_words[0].bitcast(I32))
-        nc.sync.dma_start(out=x_words[:].bitcast(I32), in_=xt_words[0].rearrange("p n t -> p (n t)").bitcast(I32))
-        load_scale_rows(nc.scalar, w_raw_bytes[:], w_scales)
-        load_scale_rows(nc.sync, x_bytes[:], xt_scales)
         nc.sync.dma_start(lists[2][:], offs3)
+        load_scale_rows([nc.sync, nc.sync, nc.scalar, nc.scalar], w_raw_bytes[:], w_scales)
+        nc.sync.dma_start(out=x_words[:].bitcast(I32), in_=xt_words[0].rearrange("p n t -> p (n t)").bitcast(I32))
+        nc.sync.dma_start(out=w_raw[:].bitcast(I32), in_=w_words[0].bitcast(I32))
+        load_scale_rows(sync4, x_bytes[:], xt_scales)
         nc.sync.dma_start(lists[1][:], offs2)
         nc.sync.dma_start(lists[3][:], offs4)
-        nc.sync.dma_start(out=ws_sb[:].bitcast(I32), in_=ws_words[0].rearrange("p n t -> p (n t)").bitcast(I32))
-        load_scale_rows(nc.sync, o_bytes[:, N : 2 * N], ws_scales)
         nc.sync.dma_start(lists[4][:], offs5)
         for h in range(2):
             nc.sync.dma_start(out=tz_sb[h][:], in_=tz[P * h : P * (h + 1), :])
+        nc.sync.dma_start(out=ws_sb[:].bitcast(I32), in_=ws_words[0].rearrange("p n t -> p (n t)").bitcast(I32))
         nc.sync.dma_start(out=wb_sb[:].bitcast(I32), in_=wb_words[0].rearrange("p n t -> p (n t)").bitcast(I32))
-        load_scale_rows(nc.sync, o_bytes[:, 0:N], wb_scales)
+        load_scale_rows(sync4, o_bytes[:, N : 2 * N], ws_scales)
+        load_scale_rows(sync4, o_bytes[:, 0:N], wb_scales)
 
         w_sb = tile([P, 2 * R], U8, "w_sb")
         w_bytes = tile([P, R], U8, "w_bytes")
@@ -78,63 +81,77 @@ def tile_list_tied_board_skip_tabled_kernel(tc, xt_words, xt_scales, w_words, w_
         g_words = [tile([P, J], U32, "g_words%d" % i) for i in range(2)]
         g_bytes = [tile([P, J], U8, "g_bytes%d" % i) for i in range(2)]
 
-        def first_matrix(dst, t, i):
+        def first_matrix(dst, t, i, cols):
             nc.tensor.matmul_mx(out=dst, lhsT=w_sb[:, 2 * P * t : 2 * P * (t + 1)].bitcast(E2M1),
                                 lhsT_scale=w_bytes[:, P * t : P * (t + 1)],
-                                rhs=g_words[i][:].bitcast(E4M3), rhs_scale=g_bytes[i][:], start=True, stop=True)
+                                rhs=g_words[i][:, cols].bitcast(E4M3), rhs_scale=g_bytes[i][:, cols], start=True, stop=True)
 
-        nc.vector.tensor_copy(g_bytes[0][:], x_bytes[:].indirect(lists[0][:]))
+        halves = [slice(0, HALF), slice(HALF, J)]
         nc.vector.tensor_copy(g_words[0][:], x_words[:].indirect(lists[0][:]))
+        nc.vector.tensor_copy(g_bytes[0][:], x_bytes[:].indirect(lists[0][:]))
         a_ps = [ps.tile([P, J], F32, name="a_ps%d" % t) for t in range(PACK)]
         for t in range(PACK):
-            first_matrix(a_ps[t][:], t, 0)
-
-        nc.vector.tensor_copy(g_bytes[1][:], x_bytes[:].indirect(lists[1][:]))
-        nc.vector.tensor_copy(g_words[1][:], x_words[:].indirect(lists[1][:]))
-        b_ps = [ps.tile([P, 2, J], F32, name="b_ps%d" % u) for u in range(2)]
-        for t in range(PACK):
-            first_matrix(b_ps[t // 2][:, t % 2, :], t, 1)
-        p_ps = [ps.tile([P, J], F32, name="p_ps%d" % h) for h in range(2)]
-        for h in range(2):
-            nc.tensor.matmul_mx(out=p_ps[h][:], lhsT=ws_sb[:, P * h : P * (h + 1)].bitcast(E5M2),
-                                lhsT_scale=o_bytes[:, N + P * h : N + P * (h + 1)],
-                                rhs=g_words[1][:].bitcast(E4M3), rhs_scale=g_bytes[1][:], start=True, stop=False)
+            first_matrix(a_ps[t][:], t, 0, slice(0, J))
 
         a_sb = [tile([P, J], F32, "a_sb%d" % t) for t in range(PACK)]
-        seen = [tile([P, J], F32, "seen%d" % t) for t in range(PACK)]
-        diff = tile([P, PACK, J], F32, "diff")
-        for t in range(PACK):
+        seen = tile([P, PACK, J], F32, "seen")
+
+        def put(t):
             if t % 2 == 0:
                 nc.scalar.copy(out=a_sb[t][:], in_=a_ps[t][:])
                 nc.scalar.activation(board[t][:].indirect(lists[2][:]), a_sb[t][:], ACT.Copy)
             else:
                 nc.vector.tensor_copy(out=a_sb[t][:], in_=a_ps[t][:])
                 nc.vector.tensor_copy(board[t][:].indirect(lists[2][:]), a_sb[t][:])
+
+        put(0)
+        put(1)
+        nc.vector.tensor_copy(g_bytes[1][:], x_bytes[:].indirect(lists[1][:]))
+        nc.vector.tensor_copy(g_words[1][:], x_words[:].indirect(lists[1][:]))
+        put(2)
+        put(3)
+        b_ps = [ps.tile([P, PACK, HALF], F32, name="b_ps%d" % u) for u in range(2)]
+        for u in range(2):
+            for t in range(PACK):
+                first_matrix(b_ps[u][:, t, :], t, 1, halves[u])
+        p_ps = [ps.tile([P, 2, HALF], F32, name="p_ps%d" % u) for u in range(2)]
+        for u in range(2):
+            for h in range(2):
+                nc.tensor.matmul_mx(out=p_ps[u][:, h, :], lhsT=ws_sb[:, P * h : P * (h + 1)].bitcast(E5M2),
+                                    lhsT_scale=o_bytes[:, N + P * h : N + P * (h + 1)],
+                                    rhs=g_words[1][:, halves[u]].bitcast(E4M3), rhs_scale=g_bytes[1][:, halves[u]],
+                                    start=(h == 0), stop=False)
+
         for t in range(PACK):
-            if t % 2 == 0:
-                nc.scalar.activation(seen[t][:], board[t][:].indirect(lists[3][:]), ACT.Copy)
+            if t < 2:
+                nc.scalar.activation(seen[:, t, :], board[t][:].indirect(lists[3][:]), ACT.Copy)
             else:
-                nc.vector.tensor_copy(seen[t][:], board[t][:].indirect(lists[3][:]))
-        for t in range(PACK):
-            nc.vector.tensor_tensor(out=diff[:, t, :], in0=seen[t][:], in1=b_ps[t // 2][:, t % 2, :], op=ALU.subtract)
+                nc.vector.tensor_copy(seen[:, t, :], board[t][:].indirect(lists[3][:]))
 
-        hid = tile([P, J, PACK], BF16, "hid")
-        half = J // 2
-        nc.scalar.activation(out=hid[:, 0:half, :], in_=diff[:, :, 0:half].rearrange("p t j -> p j t"), func=ACT.Abs)
-        upper = diff[:, :, half:J].rearrange("p t j -> p j t")
-        nc.vector.scalar_tensor_tensor(out=hid[:, half:J, :], in0=upper, scalar=-1.0, in1=upper, op0=ALU.mult, op1=ALU.max)
-        h_words = tile([P, J], U32, "h_words")
-        h_bytes = tile([P, J], U8, "h_bytes")
-        nc.vector.quantize_mx(out=h_words[:].bitcast(E4M3), scales=h_bytes[:], in_=hid[:].rearrange("p j t -> p (j t)"))
+        diff = [tile([P, PACK, HALF], F32, "diff%d" % u) for u in range(2)]
+        hid = [tile([P, HALF, PACK], BF16, "hid%d" % u) for u in range(2)]
+        for u in range(2):
+            nc.vector.tensor_tensor(out=diff[u][:], in0=seen[:, :, halves[u]], in1=b_ps[u][:], op=ALU.subtract)
+        nc.scalar.activation(out=hid[0][:], in_=diff[0][:].rearrange("p t j -> p j t"), func=ACT.Abs)
+        nc.scalar.activation(out=hid[1][:, 0:CUT, :], in_=diff[1][:, :, 0:CUT].rearrange("p t j -> p j t"), func=ACT.Abs)
+        upper = diff[1][:, :, CUT:HALF].rearrange("p t j -> p j t")
+        nc.vector.scalar_tensor_tensor(out=hid[1][:, CUT:HALF, :], in0=upper, scalar=-1.0, in1=upper, op0=ALU.mult, op1=ALU.max)
 
-        picked = [tile([P, J], F32, "picked%d" % h) for h in range(2)]
-        res = [tile([P, J], F32, "res%d" % h) for h in range(2)]
+        picked = tile([P, 2, J], F32, "picked")
         for h in range(2):
-            nc.tensor.matmul_mx(out=p_ps[h][:], lhsT=wb_sb[:, P * h : P * (h + 1)].bitcast(E5M2),
-                                lhsT_scale=o_bytes[:, P * h : P * (h + 1)],
-                                rhs=h_words[:].bitcast(E4M3), rhs_scale=h_bytes[:], start=False, stop=True)
-        for h in range(2):
-            nc.scalar.activation(picked[h][:], tz_sb[h][:].indirect(lists[4][:]), ACT.Copy)
-        for h in range(2):
-            nc.vector.tensor_tensor(out=res[h][:], in0=p_ps[h][:], in1=picked[h][:], op=ALU.add)
-            (nc.sync, nc.scalar)[h].dma_start(out=out[P * h : P * (h + 1), :], in_=res[h][:])
+            nc.scalar.activation(picked[:, h, :], tz_sb[h][:].indirect(lists[4][:]), ACT.Copy)
+
+        h_words = [tile([P, HALF], U32, "h_words%d" % u) for u in range(2)]
+        h_bytes = [tile([P, HALF], U8, "h_bytes%d" % u) for u in range(2)]
+        res = [tile([P, 2, HALF], F32, "res%d" % u) for u in range(2)]
+        for u in range(2):
+            nc.vector.quantize_mx(out=h_words[u][:].bitcast(E4M3), scales=h_bytes[u][:],
+                                  in_=hid[u][:].rearrange("p j t -> p (j t)"))
+            for h in range(2):
+                nc.tensor.matmul_mx(out=p_ps[u][:, h, :], lhsT=wb_sb[:, P * h : P * (h + 1)].bitcast(E5M2),
+                                    lhsT_scale=o_bytes[:, P * h : P * (h + 1)],
+                                    rhs=h_words[u][:].bitcast(E4M3), rhs_scale=h_bytes[u][:], start=False, stop=(h == 1))
+        out_rows = out.rearrange("(h p) j -> p h j", p=P)
+        for u in range(2):
+            nc.vector.tensor_tensor(out=res[u][:], in0=p_ps[u][:], in1=picked[:, :, halves[u]], op=ALU.add)
+            (nc.sync, nc.scalar)[u].dma_start(out=out_rows[:, :, halves[u]], in_=res[u][:])

@@ -16,15 +16,24 @@ E5M2 = mybir.dt.float8_e5m2_x4
 E2M1 = mybir.dt.float4_e2m1fn_x4
 ACT = mybir.ActivationFunctionType
 ALU = mybir.AluOpType
+
 P = 128
 PACK = 4
+QUADRANTS = 4
+LIST_COLS = J // 16
 HALF = J // 2
-CUT = 64
+N_TILES = N // P
+SCALAR_SLOTS = 96
 
 
 def load_scale_rows(queues, plane, scales):
-    for q in range(4):
-        queues[q].dma_start(out=plane[32 * q : 32 * q + 4, :].bitcast(I32), in_=scales[0, 4 * q : 4 * q + 4, :].bitcast(I32))
+    for q in range(QUADRANTS):
+        queues[q].dma_start(out=plane[32 * q : 32 * q + 4, :].bitcast(I32),
+                            in_=scales[0, 4 * q : 4 * q + 4, :].bitcast(I32))
+
+
+def as_words(packed):
+    return packed[0].rearrange("p n t -> p (n t)").bitcast(I32)
 
 
 def tile_list_tied_board_skip_tabled_kernel(tc, xt_words, xt_scales, w_words, w_scales, wb_words, wb_scales,
@@ -37,7 +46,7 @@ def tile_list_tied_board_skip_tabled_kernel(tc, xt_words, xt_scales, w_words, w_
         def tile(shape, dtype, name):
             return sb.tile(shape, dtype, name=name, align_bytes=64)
 
-        lists = [sb.tile([P, J // 16], U16, name="list%d" % i) for i in range(5)]
+        idx, idx2, idx3, idx4, idx5 = [sb.tile([P, LIST_COLS], U16, name="list%d" % i) for i in range(5)]
         x_words = tile([P, T], U32, "x_words")
         x_bytes = tile([P, T], U8, "x_bytes")
         w_raw = tile([P, 2 * R], U8, "w_raw")
@@ -45,31 +54,31 @@ def tile_list_tied_board_skip_tabled_kernel(tc, xt_words, xt_scales, w_words, w_
         o_bytes = tile([P, 2 * N], U8, "o_bytes")
         wb_sb = tile([P, N], U32, "wb_sb")
         ws_sb = tile([P, N], U32, "ws_sb")
-        tz_sb = [tile([P, E], F32, "tz%d" % h) for h in range(2)]
+        tz_sb = [tile([P, E], F32, "tz%d" % h) for h in range(N_TILES)]
         board = [tile([P, C], F32, "board%d" % t) for t in range(PACK)]
 
         nc.vector.memset(w_raw_bytes[:].bitcast(I32), 0)
         nc.vector.memset(x_bytes[:].bitcast(I32), 0)
-        nc.gpsimd.memset(o_bytes[:].bitcast(I32), 0)
+        nc.vector.memset(o_bytes[:].bitcast(I32), 0)
         for t in range(PACK):
             nc.vector.memset(board[t][:], 0.0)
 
-        sync4 = [nc.sync] * 4
-        nc.sync.dma_start(lists[0][:], offs)
-        nc.sync.dma_start(lists[2][:], offs3)
+        on_sync = [nc.sync] * QUADRANTS
+        nc.sync.dma_start(idx[:], offs)
+        nc.sync.dma_start(idx3[:], offs3)
         load_scale_rows([nc.sync, nc.sync, nc.scalar, nc.scalar], w_raw_bytes[:], w_scales)
-        nc.sync.dma_start(out=x_words[:].bitcast(I32), in_=xt_words[0].rearrange("p n t -> p (n t)").bitcast(I32))
+        nc.sync.dma_start(out=x_words[:].bitcast(I32), in_=as_words(xt_words))
         nc.sync.dma_start(out=w_raw[:].bitcast(I32), in_=w_words[0].bitcast(I32))
-        load_scale_rows(sync4, x_bytes[:], xt_scales)
-        nc.sync.dma_start(lists[1][:], offs2)
-        nc.sync.dma_start(lists[3][:], offs4)
-        nc.sync.dma_start(lists[4][:], offs5)
-        for h in range(2):
+        load_scale_rows(on_sync, x_bytes[:], xt_scales)
+        nc.sync.dma_start(idx2[:], offs2)
+        nc.sync.dma_start(idx4[:], offs4)
+        nc.sync.dma_start(idx5[:], offs5)
+        for h in range(N_TILES):
             nc.sync.dma_start(out=tz_sb[h][:], in_=tz[P * h : P * (h + 1), :])
-        nc.sync.dma_start(out=ws_sb[:].bitcast(I32), in_=ws_words[0].rearrange("p n t -> p (n t)").bitcast(I32))
-        nc.sync.dma_start(out=wb_sb[:].bitcast(I32), in_=wb_words[0].rearrange("p n t -> p (n t)").bitcast(I32))
-        load_scale_rows(sync4, o_bytes[:, N : 2 * N], ws_scales)
-        load_scale_rows(sync4, o_bytes[:, 0:N], wb_scales)
+        nc.sync.dma_start(out=ws_sb[:].bitcast(I32), in_=as_words(ws_words))
+        nc.sync.dma_start(out=wb_sb[:].bitcast(I32), in_=as_words(wb_words))
+        load_scale_rows(on_sync, o_bytes[:, N : 2 * N], ws_scales)
+        load_scale_rows(on_sync, o_bytes[:, 0:N], wb_scales)
 
         w_sb = tile([P, 2 * R], U8, "w_sb")
         w_bytes = tile([P, R], U8, "w_bytes")
@@ -81,16 +90,18 @@ def tile_list_tied_board_skip_tabled_kernel(tc, xt_words, xt_scales, w_words, w_
         g_words = [tile([P, J], U32, "g_words%d" % i) for i in range(2)]
         g_bytes = [tile([P, J], U8, "g_bytes%d" % i) for i in range(2)]
 
-        def first_matrix(dst, t, i, cols):
+        def first_matrix(dst, t, i, slots):
             nc.tensor.matmul_mx(out=dst, lhsT=w_sb[:, 2 * P * t : 2 * P * (t + 1)].bitcast(E2M1),
                                 lhsT_scale=w_bytes[:, P * t : P * (t + 1)],
-                                rhs=g_words[i][:, cols].bitcast(E4M3), rhs_scale=g_bytes[i][:, cols], start=True, stop=True)
+                                rhs=g_words[i][:, slots].bitcast(E4M3), rhs_scale=g_bytes[i][:, slots],
+                                start=True, stop=True)
 
         halves = [slice(0, HALF), slice(HALF, J)]
-        nc.vector.tensor_copy(g_words[0][:], x_words[:].indirect(lists[0][:]))
-        nc.vector.tensor_copy(g_bytes[0][:], x_bytes[:].indirect(lists[0][:]))
+        nc.vector.tensor_copy(g_words[0][:], x_words[:].indirect(idx[:]))
+        nc.vector.tensor_copy(g_bytes[0][:], x_bytes[:].indirect(idx[:]))
+
         a_ps = [ps.tile([P, J], F32, name="a_ps%d" % t) for t in range(PACK)]
-        for t in range(PACK):
+        for t in (0, 2, 1, 3):
             first_matrix(a_ps[t][:], t, 0, slice(0, J))
 
         a_sb = [tile([P, J], F32, "a_sb%d" % t) for t in range(PACK)]
@@ -99,58 +110,65 @@ def tile_list_tied_board_skip_tabled_kernel(tc, xt_words, xt_scales, w_words, w_
         def put(t):
             if t % 2 == 0:
                 nc.scalar.copy(out=a_sb[t][:], in_=a_ps[t][:])
-                nc.scalar.activation(board[t][:].indirect(lists[2][:]), a_sb[t][:], ACT.Copy)
+                nc.scalar.activation(board[t][:].indirect(idx3[:]), a_sb[t][:], ACT.Copy)
             else:
                 nc.vector.tensor_copy(out=a_sb[t][:], in_=a_ps[t][:])
-                nc.vector.tensor_copy(board[t][:].indirect(lists[2][:]), a_sb[t][:])
+                nc.vector.tensor_copy(board[t][:].indirect(idx3[:]), a_sb[t][:])
 
         put(0)
         put(1)
-        nc.vector.tensor_copy(g_bytes[1][:], x_bytes[:].indirect(lists[1][:]))
-        nc.vector.tensor_copy(g_words[1][:], x_words[:].indirect(lists[1][:]))
+        nc.vector.tensor_copy(g_bytes[1][:], x_bytes[:].indirect(idx2[:]))
+        nc.vector.tensor_copy(g_words[1][:], x_words[:].indirect(idx2[:]))
         put(2)
         put(3)
+
         b_ps = [ps.tile([P, PACK, HALF], F32, name="b_ps%d" % u) for u in range(2)]
         for u in range(2):
             for t in range(PACK):
                 first_matrix(b_ps[u][:, t, :], t, 1, halves[u])
-        p_ps = [ps.tile([P, 2, HALF], F32, name="p_ps%d" % u) for u in range(2)]
+
+        p_ps = [ps.tile([P, N_TILES, HALF], F32, name="p_ps%d" % u) for u in range(2)]
         for u in range(2):
-            for h in range(2):
+            for h in range(N_TILES):
                 nc.tensor.matmul_mx(out=p_ps[u][:, h, :], lhsT=ws_sb[:, P * h : P * (h + 1)].bitcast(E5M2),
                                     lhsT_scale=o_bytes[:, N + P * h : N + P * (h + 1)],
                                     rhs=g_words[1][:, halves[u]].bitcast(E4M3), rhs_scale=g_bytes[1][:, halves[u]],
                                     start=(h == 0), stop=False)
 
-        for t in range(PACK):
-            if t < 2:
-                nc.scalar.activation(seen[:, t, :], board[t][:].indirect(lists[3][:]), ACT.Copy)
-            else:
-                nc.vector.tensor_copy(seen[:, t, :], board[t][:].indirect(lists[3][:]))
+        idx4_half = [idx4[:, 0 : LIST_COLS // 2], idx4[:, LIST_COLS // 2 : LIST_COLS]]
+        nc.scalar.activation(seen[:, 0, :], board[0][:].indirect(idx4[:]), ACT.Copy)
+        for t, u in ((1, 0), (2, 0), (2, 1)):
+            nc.scalar.activation(seen[:, t, halves[u]], board[t][:].indirect(idx4_half[u]), ACT.Copy)
+        for t, u in ((1, 1), (3, 0), (3, 1)):
+            nc.vector.tensor_copy(seen[:, t, halves[u]], board[t][:].indirect(idx4_half[u]))
 
         diff = [tile([P, PACK, HALF], F32, "diff%d" % u) for u in range(2)]
         hid = [tile([P, HALF, PACK], BF16, "hid%d" % u) for u in range(2)]
         for u in range(2):
             nc.vector.tensor_tensor(out=diff[u][:], in0=seen[:, :, halves[u]], in1=b_ps[u][:], op=ALU.subtract)
         nc.scalar.activation(out=hid[0][:], in_=diff[0][:].rearrange("p t j -> p j t"), func=ACT.Abs)
-        nc.scalar.activation(out=hid[1][:, 0:CUT, :], in_=diff[1][:, :, 0:CUT].rearrange("p t j -> p j t"), func=ACT.Abs)
-        upper = diff[1][:, :, CUT:HALF].rearrange("p t j -> p j t")
-        nc.vector.scalar_tensor_tensor(out=hid[1][:, CUT:HALF, :], in0=upper, scalar=-1.0, in1=upper, op0=ALU.mult, op1=ALU.max)
+        nc.scalar.activation(out=hid[1][:, 0:SCALAR_SLOTS, :],
+                             in_=diff[1][:, :, 0:SCALAR_SLOTS].rearrange("p t j -> p j t"), func=ACT.Abs)
+        rest = diff[1][:, :, SCALAR_SLOTS:HALF].rearrange("p t j -> p j t")
+        nc.vector.scalar_tensor_tensor(out=hid[1][:, SCALAR_SLOTS:HALF, :], in0=rest, scalar=-1.0, in1=rest,
+                                       op0=ALU.mult, op1=ALU.max)
 
-        picked = tile([P, 2, J], F32, "picked")
-        for h in range(2):
-            nc.scalar.activation(picked[:, h, :], tz_sb[h][:].indirect(lists[4][:]), ACT.Copy)
+        picked = tile([P, N_TILES, J], F32, "picked")
+        for h in range(N_TILES):
+            nc.scalar.activation(picked[:, h, :], tz_sb[h][:].indirect(idx5[:]), ACT.Copy)
 
         h_words = [tile([P, HALF], U32, "h_words%d" % u) for u in range(2)]
         h_bytes = [tile([P, HALF], U8, "h_bytes%d" % u) for u in range(2)]
-        res = [tile([P, 2, HALF], F32, "res%d" % u) for u in range(2)]
+        res = [tile([P, N_TILES, HALF], F32, "res%d" % u) for u in range(2)]
         for u in range(2):
             nc.vector.quantize_mx(out=h_words[u][:].bitcast(E4M3), scales=h_bytes[u][:],
                                   in_=hid[u][:].rearrange("p j t -> p (j t)"))
-            for h in range(2):
+            for h in range(N_TILES):
                 nc.tensor.matmul_mx(out=p_ps[u][:, h, :], lhsT=wb_sb[:, P * h : P * (h + 1)].bitcast(E5M2),
                                     lhsT_scale=o_bytes[:, P * h : P * (h + 1)],
-                                    rhs=h_words[u][:].bitcast(E4M3), rhs_scale=h_bytes[u][:], start=False, stop=(h == 1))
+                                    rhs=h_words[u][:].bitcast(E4M3), rhs_scale=h_bytes[u][:],
+                                    start=False, stop=(h == N_TILES - 1))
+
         out_rows = out.rearrange("(h p) j -> p h j", p=P)
         for u in range(2):
             nc.vector.tensor_tensor(out=res[u][:], in0=p_ps[u][:], in1=picked[:, :, halves[u]], op=ALU.add)

from contextlib import ExitStack

import concourse.mybir as mybir

K, T, J, R, C, N, E = 512, 2048, 256, 512, 512, 256, 1024
FLOPS = 2 * J * (2 * K * R + R * N + K * N)

F32 = mybir.dt.float32
BF16 = mybir.dt.bfloat16
I32 = mybir.dt.int32
U32 = mybir.dt.uint32
U16 = mybir.dt.uint16
U8 = mybir.dt.uint8
E4M3 = mybir.dt.float8_e4m3fn_x4
E5M2 = mybir.dt.float8_e5m2_x4
E2M1 = mybir.dt.float4_e2m1fn_x4
ACT = mybir.ActivationFunctionType
ALU = mybir.AluOpType

P = 128
PACK = 4
QUADRANTS = 4
LIST_COLS = J // 16
HALF = J // 2
N_TILES = N // P
SCALAR_SLOTS = 96


def load_scale_rows(queues, plane, scales):
    for q in range(QUADRANTS):
        queues[q].dma_start(out=plane[32 * q : 32 * q + 4, :].bitcast(I32),
                            in_=scales[0, 4 * q : 4 * q + 4, :].bitcast(I32))


def as_words(packed):
    return packed[0].rearrange("p n t -> p (n t)").bitcast(I32)


def tile_list_tied_board_skip_tabled_kernel(tc, xt_words, xt_scales, w_words, w_scales, wb_words, wb_scales,
                                                ws_words, ws_scales, tz, offs, offs2, offs3, offs4, offs5, out):
    nc = tc.nc
    with ExitStack() as ctx:
        sb = ctx.enter_context(tc.tile_pool(name="sb", bufs=1))
        ps = ctx.enter_context(tc.psum_pool(name="ps", bufs=1))

        def tile(shape, dtype, name):
            return sb.tile(shape, dtype, name=name, align_bytes=64)

        idx, idx2, idx3, idx4, idx5 = [sb.tile([P, LIST_COLS], U16, name="list%d" % i) for i in range(5)]
        x_words = tile([P, T], U32, "x_words")
        x_bytes = tile([P, T], U8, "x_bytes")
        w_raw = tile([P, 2 * R], U8, "w_raw")
        w_raw_bytes = tile([P, R], U8, "w_raw_bytes")
        o_bytes = tile([P, 2 * N], U8, "o_bytes")
        wb_sb = tile([P, N], U32, "wb_sb")
        ws_sb = tile([P, N], U32, "ws_sb")
        tz_sb = [tile([P, E], F32, "tz%d" % h) for h in range(N_TILES)]
        board = [tile([P, C], F32, "board%d" % t) for t in range(PACK)]

        nc.vector.memset(w_raw_bytes[:].bitcast(I32), 0)
        nc.vector.memset(x_bytes[:].bitcast(I32), 0)
        nc.vector.memset(o_bytes[:].bitcast(I32), 0)
        for t in range(PACK):
            nc.vector.memset(board[t][:], 0.0)

        on_sync = [nc.sync] * QUADRANTS
        nc.sync.dma_start(idx[:], offs)
        nc.sync.dma_start(idx3[:], offs3)
        load_scale_rows([nc.sync, nc.sync, nc.scalar, nc.scalar], w_raw_bytes[:], w_scales)
        nc.sync.dma_start(out=x_words[:].bitcast(I32), in_=as_words(xt_words))
        nc.sync.dma_start(out=w_raw[:].bitcast(I32), in_=w_words[0].bitcast(I32))
        load_scale_rows(on_sync, x_bytes[:], xt_scales)
        nc.sync.dma_start(idx2[:], offs2)
        nc.sync.dma_start(idx4[:], offs4)
        nc.sync.dma_start(idx5[:], offs5)
        for h in range(N_TILES):
            nc.sync.dma_start(out=tz_sb[h][:], in_=tz[P * h : P * (h + 1), :])
        nc.sync.dma_start(out=ws_sb[:].bitcast(I32), in_=as_words(ws_words))
        nc.sync.dma_start(out=wb_sb[:].bitcast(I32), in_=as_words(wb_words))
        load_scale_rows(on_sync, o_bytes[:, N : 2 * N], ws_scales)
        load_scale_rows(on_sync, o_bytes[:, 0:N], wb_scales)

        w_sb = tile([P, 2 * R], U8, "w_sb")
        w_bytes = tile([P, R], U8, "w_bytes")
        nc.scalar.copy(out=w_sb[:].bitcast(U16).rearrange("p (t m) -> p t m", t=PACK),
                       in_=w_raw[:].bitcast(U16).rearrange("p (m t) -> p t m", t=PACK))
        nc.vector.tensor_copy(out=w_bytes[:].rearrange("p (t m) -> p t m", t=PACK),
                              in_=w_raw_bytes[:].rearrange("p (m t) -> p t m", t=PACK))

        g_words = [tile([P, J], U32, "g_words%d" % i) for i in range(2)]
        g_bytes = [tile([P, J], U8, "g_bytes%d" % i) for i in range(2)]

        def first_matrix(dst, t, i, slots):
            nc.tensor.matmul_mx(out=dst, lhsT=w_sb[:, 2 * P * t : 2 * P * (t + 1)].bitcast(E2M1),
                                lhsT_scale=w_bytes[:, P * t : P * (t + 1)],
                                rhs=g_words[i][:, slots].bitcast(E4M3), rhs_scale=g_bytes[i][:, slots],
                                start=True, stop=True)

        halves = [slice(0, HALF), slice(HALF, J)]
        nc.vector.tensor_copy(g_words[0][:], x_words[:].indirect(idx[:]))
        nc.vector.tensor_copy(g_bytes[0][:], x_bytes[:].indirect(idx[:]))

        a_ps = [ps.tile([P, J], F32, name="a_ps%d" % t) for t in range(PACK)]
        for t in (0, 2, 1, 3):
            first_matrix(a_ps[t][:], t, 0, slice(0, J))

        a_sb = [tile([P, J], F32, "a_sb%d" % t) for t in range(PACK)]
        seen = tile([P, PACK, J], F32, "seen")

        def put(t):
            if t % 2 == 0:
                nc.scalar.copy(out=a_sb[t][:], in_=a_ps[t][:])
                nc.scalar.activation(board[t][:].indirect(idx3[:]), a_sb[t][:], ACT.Copy)
            else:
                nc.vector.tensor_copy(out=a_sb[t][:], in_=a_ps[t][:])
                nc.vector.tensor_copy(board[t][:].indirect(idx3[:]), a_sb[t][:])

        put(0)
        put(1)
        nc.vector.tensor_copy(g_bytes[1][:], x_bytes[:].indirect(idx2[:]))
        nc.vector.tensor_copy(g_words[1][:], x_words[:].indirect(idx2[:]))
        put(2)
        put(3)

        b_ps = [ps.tile([P, PACK, HALF], F32, name="b_ps%d" % u) for u in range(2)]
        for u in range(2):
            for t in range(PACK):
                first_matrix(b_ps[u][:, t, :], t, 1, halves[u])

        p_ps = [ps.tile([P, N_TILES, HALF], F32, name="p_ps%d" % u) for u in range(2)]
        for u in range(2):
            for h in range(N_TILES):
                nc.tensor.matmul_mx(out=p_ps[u][:, h, :], lhsT=ws_sb[:, P * h : P * (h + 1)].bitcast(E5M2),
                                    lhsT_scale=o_bytes[:, N + P * h : N + P * (h + 1)],
                                    rhs=g_words[1][:, halves[u]].bitcast(E4M3), rhs_scale=g_bytes[1][:, halves[u]],
                                    start=(h == 0), stop=False)

        idx4_half = [idx4[:, 0 : LIST_COLS // 2], idx4[:, LIST_COLS // 2 : LIST_COLS]]
        nc.scalar.activation(seen[:, 0, :], board[0][:].indirect(idx4[:]), ACT.Copy)
        for t, u in ((1, 0), (2, 0), (2, 1)):
            nc.scalar.activation(seen[:, t, halves[u]], board[t][:].indirect(idx4_half[u]), ACT.Copy)
        for t, u in ((1, 1), (3, 0), (3, 1)):
            nc.vector.tensor_copy(seen[:, t, halves[u]], board[t][:].indirect(idx4_half[u]))

        diff = [tile([P, PACK, HALF], F32, "diff%d" % u) for u in range(2)]
        hid = [tile([P, HALF, PACK], BF16, "hid%d" % u) for u in range(2)]
        for u in range(2):
            nc.vector.tensor_tensor(out=diff[u][:], in0=seen[:, :, halves[u]], in1=b_ps[u][:], op=ALU.subtract)
        nc.scalar.activation(out=hid[0][:], in_=diff[0][:].rearrange("p t j -> p j t"), func=ACT.Abs)
        nc.scalar.activation(out=hid[1][:, 0:SCALAR_SLOTS, :],
                             in_=diff[1][:, :, 0:SCALAR_SLOTS].rearrange("p t j -> p j t"), func=ACT.Abs)
        rest = diff[1][:, :, SCALAR_SLOTS:HALF].rearrange("p t j -> p j t")
        nc.vector.scalar_tensor_tensor(out=hid[1][:, SCALAR_SLOTS:HALF, :], in0=rest, scalar=-1.0, in1=rest,
                                       op0=ALU.mult, op1=ALU.max)

        picked = tile([P, N_TILES, J], F32, "picked")
        for h in range(N_TILES):
            nc.scalar.activation(picked[:, h, :], tz_sb[h][:].indirect(idx5[:]), ACT.Copy)

        h_words = [tile([P, HALF], U32, "h_words%d" % u) for u in range(2)]
        h_bytes = [tile([P, HALF], U8, "h_bytes%d" % u) for u in range(2)]
        res = [tile([P, N_TILES, HALF], F32, "res%d" % u) for u in range(2)]
        for u in range(2):
            nc.vector.quantize_mx(out=h_words[u][:].bitcast(E4M3), scales=h_bytes[u][:],
                                  in_=hid[u][:].rearrange("p j t -> p (j t)"))
            for h in range(N_TILES):
                nc.tensor.matmul_mx(out=p_ps[u][:, h, :], lhsT=wb_sb[:, P * h : P * (h + 1)].bitcast(E5M2),
                                    lhsT_scale=o_bytes[:, P * h : P * (h + 1)],
                                    rhs=h_words[u][:].bitcast(E4M3), rhs_scale=h_bytes[u][:],
                                    start=False, stop=(h == N_TILES - 1))

        out_rows = out.rearrange("(h p) j -> p h j", p=P)
        for u in range(2):
            nc.vector.tensor_tensor(out=res[u][:], in0=p_ps[u][:], in1=picked[:, :, halves[u]], op=ALU.add)
            (nc.sync, nc.scalar)[u].dma_start(out=out_rows[:, :, halves[u]], in_=res[u][:])
